import numpy as np, ml_dtypes
CORES = [0,1,2,3,4,5,6,7]
N = 8
ROOT = 5
def setup_inputs(rng):
    return {"x": rng.standard_normal((N, 128, 8), dtype=np.float32).astype(ml_dtypes.bfloat16)}
def reference(x):
    return {"y": np.broadcast_to(x[ROOT], x.shape)}

from concourse.bass import DstId, RemoteDMATransfer

SCRATCH = {
    "stage": ("dram", [128, 8], "bfloat16"),
    "land": ("dram", [128, 8], "bfloat16"),
}
SEMAPHORES = ["loaded", "sent", "arrived", "stored"]

MASK = 0xFFFF
ENGINES = 16


def rank_program(g, core, T, topo):
    rank = T.rank_of(core)
    if rank is None:
        return
    root = T.cores[T.root]

    if core == root:
        g.sync.dma_start(T.stage[:], T.x[:]).then_inc(T.sem.loaded, 16)
        g.scalar.dma_start(T.y[:], T.x[:]).then_inc(T.sem.stored, 16)
        others = [c for c in T.cores if c != root]
        ids = []
        for c in others:
            rid, pid, _se = topo.addr(c)
            ids.append(DstId(rid=rid, pnc=pid))
        g.wait_ge(T.sem.loaded, 16)
        g.remote_dma_fused(
            [RemoteDMATransfer(dst_ids=ids, dma_engine_mask=MASK, remote_sem=T.sem.arrived,
                               srcs=[T.stage[:]], dsts=[T.land[:] for _c in others], alu_op=0)],
            local_sem=T.sem.sent)
        g.wait_ge(T.sem.sent, ENGINES)
        g.wait_ge(T.sem.stored, 16)
    else:
        g.sync.wait_ge(T.sem.arrived, ENGINES)
        g.sync.dma_start(T.y[:], T.land[:]).then_inc(T.sem.stored, 16)
        g.wait_ge(T.sem.stored, 16)
